import numpy as np, ml_dtypes
CORES = [16,23,24,31,64,71]
N = 6
import mx_ref
NC, ROOT = 128, 5
BF = ml_dtypes.bfloat16
def cut(t, i, w=512):
    return t[:, w * i:w * i + w]
def term(a, B):
    return np.stack([np.maximum(mx_ref.matmul(mx_ref.quantize(cut(a, i)), B), 0) for i in range(4)], axis=2).reshape(128, -1)
def setup_inputs(rng):
    def f(*shape):
        return mx_ref.flush((rng.standard_normal(shape, dtype=np.float32) * np.exp2(rng.integers(-2, 3, shape[:-1] + (1,)))).astype(BF))
    return {"a": f(N, 128, 4 * 512), "b": f(N, 128, 4 * NC)}
def setup_inputs_blocks(rng):
    d = setup_inputs(rng)
    for k in ("a", "b"): d[k] = mx_ref.spread(d[k], rng, 2)
    return d
def setup_inputs_wide(rng):
    d = setup_inputs(rng)
    for k in ("a", "b"): d[k] = mx_ref.flush((d[k].astype(np.float32) * np.exp2(rng.integers(-4, 5, (N, 1, 1))).astype(np.float32)).astype(BF))
    return d
def setup_inputs_lossless(rng):
    a = np.zeros((N, 128, 4 * 128, 4), np.float32)
    for r in range(N):
        k = rng.integers(0, 512, size=4 * 128)
        a[r, k // 4, np.arange(4 * 128), k % 4] = 1.0
    size = np.repeat(2.0 ** rng.integers(-4, 5, size=(1, 1, (4 * NC) // 4)), 4, axis=2)
    b = (rng.random((N, 128, 4 * NC)) < 0.8) * size
    return {"a": a.reshape(N, 128, 4 * 512).astype(BF), "b": b.astype(np.float32).astype(BF)}
def reference(a, b):
    B0 = mx_ref.quantize(b[ROOT])
    T = [term(a[r], B0) for r in range(N)]
    y = np.zeros((N, 128, 4 * NC), np.float32)
    y[:] = mx_ref.total(T)
    return {"y": y}

@@ -1,0 +1,207 @@
+from concourse.bass import DstId, RemoteDMATransfer
+from concourse.mybir import dt, AluOpType, ActivationFunctionType
+
+NCOL = 128
+W = 512
+TILES = ["B", "T0", "T1", "T2", "T3", "T4", "T5", "P", "U", "V"]
+SCRATCH = {
+    "a_in": ("sbuf", [128, 4 * W], "bfloat16"),
+    "b_in": ("sbuf", [128, W], "bfloat16"),
+    "ones": ("sbuf", [128, W + 4], "bfloat16"),
+    "pick": ("sbuf", [128, W + 4], "bfloat16"),
+    "t_mid": ("sbuf", [128, W], "bfloat16"),
+    "s_mid": ("sbuf", [128, W], "bfloat16"),
+    "y_mid": ("sbuf", [128, W], "float32"),
+    "ca": ("sbuf", [128, 4 * NCOL], "float8_e4m3fn_x4"),
+    "pa": ("sbuf", [128, 4 * NCOL], "uint8"),
+    "cs": ("sbuf", [128, 4 * NCOL], "float8_e4m3fn_x4"),
+    "ps": ("sbuf", [128, 4 * NCOL], "uint8"),
+    "acc0": ("psum", [128, 4 * 512], "float32"),
+    "acc1": ("psum", [128, 4 * 512], "float32"),
+}
+for _t in TILES:
+    SCRATCH["c" + _t] = ("sbuf", [128, NCOL], "float8_e4m3fn_x4")
+    SCRATCH["p" + _t] = ("sbuf", [128, NCOL], "uint8")
+STAGES = "tsy"
+SEMAPHORES = ["la", "lb", "one", "sel", "qs", "qa", "stored", "sent"]
+SEMAPHORES += ["q" + _t for _t in TILES] + ["arr" + _t for _t in TILES]
+SEMAPHORES += ["%s%d" % (_s, _b) for _s in STAGES for _b in range(4)]
+SEMAPHORES += ["%s_%s" % (_s, _e) for _s in STAGES for _e in ("act", "vec")]
+
+
+def _roles(T, topo):
+    cores = [int(c) for c in T.cores]
+    root = cores[T.root]
+    other = {c: [d for d in cores if d != c and topo.chip(d) == topo.chip(c)][0] for c in cores}
+    peer = other[root]
+    gates = [c for c in cores if c not in (root, peer) and all(topo.may_write(c, d) for d in cores if d != c)]
+    near = [c for c in gates if topo.may_write(peer, c)][0]
+    far = [c for c in gates if c != near][0]
+    return root, peer, near, other[near], far, other[far]
+
+
+def _plan(T, topo):
+    root, peer, near, nspoke, far, fspoke = _roles(T, topo)
+    t = {c: "T%d" % T.rank_of(c) for c in T.cores}
+
+    def engines(src, dsts):
+        m = 0xFFFF
+        for d in dsts:
+            m &= topo.mask(src, d)
+        return [e for e in range(16) if m >> e & 1]
+
+    off = engines(root, [near])
+    inner = [e for e in engines(root, [peer]) if e not in off]
+    sends = {
+        root: [("B", [([peer], off)]), ("B", [([nspoke, fspoke], off)]), ("B", [([far], off)]),
+               (t[root], [([peer], inner)])],
+        peer: [("B", [([near], engines(peer, [near]))]), ("P", [([nspoke, near], engines(peer, [near, nspoke]))])],
+        nspoke: [(t[nspoke], [([near], engines(nspoke, [near])[::2])])],
+        fspoke: [(t[fspoke], [([far], engines(fspoke, [far])[::2])])],
+        near: [(t[near], [([nspoke], engines(near, [root]))]),
+               ("V", [([fspoke, far, peer, root], engines(near, [fspoke, far, peer, root]))])],
+        far: [(t[far], [([fspoke], engines(far, [root]))]),
+              ("U", [([nspoke, near, peer, root], engines(far, [nspoke, near, peer, root]))])],
+    }
+    sums = {peer: ("P", [t[peer], t[root]]), near: ("V", [t[near], t[nspoke], "P"]), far: ("U", [t[far], t[fspoke]])}
+    ys = {root: ["U", "V"], peer: ["U", "V"],
+          near: [t[near], t[nspoke], "P", "U"], nspoke: [t[nspoke], "P", t[near], "U"],
+          far: [t[far], t[fspoke], "V"], fspoke: [t[fspoke], t[far], "V"]}
+    return sends, sums, ys
+
+
+def rank_program(g, core, T, topo):
+    rank = T.rank_of(core)
+    if rank is None:
+        return
+    sends, sums, ys = _plan(T, topo)
+    own = "T%d" % rank
+    is_root = rank == T.root
+    made = {own}
+    if is_root:
+        made.add("B")
+    if core in sums:
+        made.add(sums[core][0])
+    arrive = {}
+    for src in sends:
+        for tile, groups in sends[src]:
+            for dsts, engs in groups:
+                if core in dsts:
+                    arrive[tile] = 2 * len(engs)
+
+    def codes(t):
+        return T["c" + t][:, 0:NCOL]
+
+    def plane(t):
+        return T["p" + t][:, 0:NCOL]
+
+    def have(q, t):
+        if t in made:
+            q.wait_ge(T.sem["q" + t], 1)
+        else:
+            q.wait_ge(T.sem["arr" + t], arrive[t])
+
+    if is_root:
+        g.sync.dma_start(T.b_in[:], T.b[:, :]).then_inc(T.sem.lb, 16)
+    g.sync.dma_start(T.a_in[:], T.a[:, :]).then_inc(T.sem.la, 16)
+
+    g.vector.memset(T.ones[:], 1.0).then_inc(T.sem.one, 1)
+    g.wait_ge(T.sem.one, 1)
+    g.affine_select(T.pick[:], T.ones[:], [[-1, W + 4]], AluOpType.is_equal, 0.0, 3, 4).then_inc(T.sem.sel, 1)
+
+    if is_root:
+        g.vector.wait_ge(T.sem.lb, 16)
+        g.vector.quantize_mx(codes("B"), plane("B"), T.b_in[:]).then_inc(T.sem.qB, 1)
+    g.vector.wait_ge(T.sem.sel, 1)
+    for b in range(4):
+        c0 = b * NCOL
+        g.vector.quantize_mx(T.cs[:, c0:c0 + NCOL], T.ps[:, c0:c0 + NCOL], T.pick[:, 3 - b:3 - b + W]).then_inc(T.sem.qs, 1)
+    g.vector.wait_ge(T.sem.la, 16)
+    g.vector.quantize_mx(T.ca[:], T.pa[:], T.a_in[:]).then_inc(T.sem.qa, 1)
+
+    def bank(acc, b):
+        return acc[:, 512 * b:512 * b + NCOL]
+
+    def leave(stage, acc, out, clamp):
+        for b in (0, 2):
+            g.scalar.wait_ge(T.sem["%s%d" % (stage, b)], 1)
+            f = ActivationFunctionType.Relu if clamp else ActivationFunctionType.Copy
+            g.scalar.activation(out[:, b:W:4], bank(acc, b), f).then_inc(T.sem[stage + "_act"], 1)
+        for b in (1, 3):
+            g.vector.wait_ge(T.sem["%s%d" % (stage, b)], 1)
+            if clamp:
+                call = g.vector.tensor_scalar(out[:, b:W:4], bank(acc, b), 0.0, None, AluOpType.max)
+            else:
+                call = g.vector.tensor_copy(out[:, b:W:4], bank(acc, b))
+            call.then_inc(T.sem[stage + "_vec"], 1)
+
+    def quantise(stage, tile, mid):
+        g.vector.wait_ge(T.sem[stage + "_vec"], 2)
+        g.vector.wait_ge(T.sem[stage + "_act"], 2)
+        g.vector.quantize_mx(codes(tile), plane(tile), mid[:]).then_inc(T.sem["q" + tile], 1)
+
+    g.tensor.wait_ge(T.sem.qa, 1)
+    have(g.tensor, "B")
+    for b in range(4):
+        c0 = b * NCOL
+        g.tensor.matmul_mx(bank(T.acc0, b), T.ca[:, c0:c0 + NCOL], T.pa[:, c0:c0 + NCOL], codes("B"), plane("B"),
+                           True, True).then_inc(T.sem["t%d" % b], 1)
+    leave("t", T.acc0, T.t_mid, True)
+    quantise("t", own, T.t_mid)
+    have(g.tensor, own)
+    g.tensor.wait_ge(T.sem.qs, 4)
+
+    todo = {"s": list(sums[core][1]) if core in sums else [], "y": list(ys[core])}
+    first = {"s": True, "y": True}
+    seen = {own}
+
+    def open_into(stage, acc, t):
+        todo[stage].remove(t)
+        last = not todo[stage]
+        for b in range(4):
+            c0 = b * NCOL
+            call = g.tensor.matmul_mx(bank(acc, b), T.cs[:, c0:c0 + NCOL], T.ps[:, c0:c0 + NCOL], codes(t), plane(t),
+                                      first[stage], last)
+            if last:
+                call.then_inc(T.sem["%s%d" % (stage, b)], 1)
+        first[stage] = False
+
+    order = list(todo["s"]) + [t for t in todo["y"] if t not in todo["s"]]
+    for t in order:
+        if t not in seen:
+            seen.add(t)
+            have(g.tensor, t)
+        if t in todo["s"]:
+            open_into("s", T.acc1, t)
+        if t in todo["y"]:
+            open_into("y", T.acc0, t)
+    if core in sums:
+        leave("s", T.acc1, T.s_mid, False)
+        quantise("s", sums[core][0], T.s_mid)
+
+    leave("y", T.acc0, T.y_mid, False)
+    g.sync.wait_ge(T.sem.y_act, 2)
+    g.sync.wait_ge(T.sem.y_vec, 2)
+    g.sync.dma_start(T.y[:, :], T.y_mid[:]).then_inc(T.sem.stored, 16)
+    g.sync.wait_ge(T.sem.stored, 16)
+
+    sent = 0
+    held = set()
+    for tile, groups in sends[core]:
+        if tile not in held:
+            held.add(tile)
+            have(g, tile)
+        for is_plane in (False, True):
+            side = plane(tile) if is_plane else codes(tile).bitcast(dt.uint8)
+            transfers = []
+            for dsts, engs in groups:
+                mask = sum(1 << e for e in engs)
+                ids = []
+                for d in dsts:
+                    rid, pid, _s = topo.addr(d)
+                    ids.append(DstId(rid=rid, pnc=pid))
+                transfers.append(RemoteDMATransfer(dst_ids=ids, dma_engine_mask=mask, remote_sem=T.sem["arr" + tile],
+                                                   srcs=[side], dsts=[side] * len(dsts)))
+                sent += len(engs)
+            g.remote_dma_fused(transfers, local_sem=T.sem.sent)
+    g.wait_ge(T.sem.sent, sent)

@@ -44,28 +44,27 @@ def _plan(T, topo):
     root, peer, near, nspoke, far, fspoke = _roles(T, topo)
     t = {c: "T%d" % T.rank_of(c) for c in T.cores}
 
-    def engines(src, dsts):
-        m = 0xFFFF
-        for d in dsts:
-            m &= topo.mask(src, d)
+    def engines(src, dst):
+        m = topo.mask(src, dst)
         return [e for e in range(16) if m >> e & 1]
 
-    off = engines(root, [near])
-    inner = [e for e in engines(root, [peer]) if e not in off]
+    off = engines(root, near)
+    inner = [e for e in engines(root, peer) if e not in off]
     sends = {
-        root: [("B", [([peer], off)]), ("B", [([nspoke, fspoke], off)]), ("B", [([far], off)]),
-               (t[root], [([peer], inner)])],
-        peer: [("B", [([near], engines(peer, [near]))]), ("P", [([nspoke, near], engines(peer, [near, nspoke]))])],
-        nspoke: [(t[nspoke], [([near], engines(nspoke, [near])[::2])])],
-        fspoke: [(t[fspoke], [([far], engines(fspoke, [far])[::2])])],
-        near: [(t[near], [([nspoke], engines(near, [root]))]),
-               ("V", [([fspoke, far, peer, root], engines(near, [fspoke, far, peer, root]))])],
-        far: [(t[far], [([fspoke], engines(far, [root]))]),
-              ("U", [([nspoke, near, peer, root], engines(far, [nspoke, near, peer, root]))])],
+        root: [("B", [peer], off), ("B", [fspoke], off), ("B", [nspoke], off), ("B", [far], off),
+               (t[root], [peer], inner)],
+        peer: [("B", [near], off), ("P", [near], off), ("P", [nspoke], off), (t[peer], [root], off),
+               ("U", [root], off)],
+        nspoke: [(t[nspoke], [near], engines(nspoke, near)[::2]), (t[nspoke], [root], off), ("V", [peer], off)],
+        fspoke: [(t[fspoke], [far], engines(fspoke, far)[::2])],
+        near: [(t[near], [nspoke], off), (t[near], [root], off), ("V", [fspoke, far], off)],
+        far: [(t[far], [fspoke], off), ("U", [peer], off), ("U", [nspoke, near], off)],
     }
-    sums = {peer: ("P", [t[peer], t[root]]), near: ("V", [t[near], t[nspoke], "P"]), far: ("U", [t[far], t[fspoke]])}
-    ys = {root: ["U", "V"], peer: ["U", "V"],
-          near: [t[near], t[nspoke], "P", "U"], nspoke: [t[nspoke], "P", t[near], "U"],
+    v = [t[near], t[nspoke], "P"]
+    sums = {peer: ("P", [t[peer], t[root]]), near: ("V", v), nspoke: ("V", [t[nspoke], "P", t[near]]),
+            far: ("U", [t[far], t[fspoke]])}
+    ys = {root: [t[root], t[peer], t[nspoke], t[near], "U"], peer: ["U", "V"],
+          near: v + ["U"], nspoke: [t[nspoke], "P", t[near], "U"],
           far: [t[far], t[fspoke], "V"], fspoke: [t[fspoke], t[far], "V"]}
     return sends, sums, ys
 
@@ -84,10 +83,9 @@ def rank_program(g, core, T, topo):
         made.add(sums[core][0])
     arrive = {}
     for src in sends:
-        for tile, groups in sends[src]:
-            for dsts, engs in groups:
-                if core in dsts:
-                    arrive[tile] = 2 * len(engs)
+        for tile, dsts, engs in sends[src]:
+            if core in dsts:
+                arrive[tile] = 2 * len(engs)
 
     def codes(t):
         return T["c" + t][:, 0:NCOL]
@@ -151,34 +149,26 @@ def rank_program(g, core, T, topo):
     have(g.tensor, own)
     g.tensor.wait_ge(T.sem.qs, 4)
 
-    todo = {"s": list(sums[core][1]) if core in sums else [], "y": list(ys[core])}
-    first = {"s": True, "y": True}
     seen = {own}
 
-    def open_into(stage, acc, t):
-        todo[stage].remove(t)
-        last = not todo[stage]
-        for b in range(4):
-            c0 = b * NCOL
-            call = g.tensor.matmul_mx(bank(acc, b), T.cs[:, c0:c0 + NCOL], T.ps[:, c0:c0 + NCOL], codes(t), plane(t),
-                                      first[stage], last)
-            if last:
-                call.then_inc(T.sem["%s%d" % (stage, b)], 1)
-        first[stage] = False
+    def add_up(stage, acc, parts):
+        for k, t in enumerate(parts):
+            if t not in seen:
+                seen.add(t)
+                have(g.tensor, t)
+            for b in range(4):
+                c0 = b * NCOL
+                call = g.tensor.matmul_mx(bank(acc, b), T.cs[:, c0:c0 + NCOL], T.ps[:, c0:c0 + NCOL], codes(t), plane(t),
+                                          k == 0, k == len(parts) - 1)
+                if k == len(parts) - 1:
+                    call.then_inc(T.sem["%s%d" % (stage, b)], 1)
 
-    order = list(todo["s"]) + [t for t in todo["y"] if t not in todo["s"]]
-    for t in order:
-        if t not in seen:
-            seen.add(t)
-            have(g.tensor, t)
-        if t in todo["s"]:
-            open_into("s", T.acc1, t)
-        if t in todo["y"]:
-            open_into("y", T.acc0, t)
     if core in sums:
+        add_up("s", T.acc1, sums[core][1])
         leave("s", T.acc1, T.s_mid, False)
         quantise("s", sums[core][0], T.s_mid)
 
+    add_up("y", T.acc0, ys[core])
     leave("y", T.acc0, T.y_mid, False)
     g.sync.wait_ge(T.sem.y_act, 2)
     g.sync.wait_ge(T.sem.y_vec, 2)
@@ -187,21 +177,17 @@ def rank_program(g, core, T, topo):
 
     sent = 0
     held = set()
-    for tile, groups in sends[core]:
+    for tile, dsts, engs in sends[core]:
         if tile not in held:
             held.add(tile)
             have(g, tile)
-        for is_plane in (False, True):
-            side = plane(tile) if is_plane else codes(tile).bitcast(dt.uint8)
-            transfers = []
-            for dsts, engs in groups:
-                mask = sum(1 << e for e in engs)
-                ids = []
-                for d in dsts:
-                    rid, pid, _s = topo.addr(d)
-                    ids.append(DstId(rid=rid, pnc=pid))
-                transfers.append(RemoteDMATransfer(dst_ids=ids, dma_engine_mask=mask, remote_sem=T.sem["arr" + tile],
-                                                   srcs=[side], dsts=[side] * len(dsts)))
-                sent += len(engs)
-            g.remote_dma_fused(transfers, local_sem=T.sem.sent)
+        ids = []
+        for d in dsts:
+            rid, pid, _s = topo.addr(d)
+            ids.append(DstId(rid=rid, pnc=pid))
+        mask = sum(1 << e for e in engs)
+        for side in (codes(tile).bitcast(dt.uint8), plane(tile)):
+            g.remote_dma_fused([RemoteDMATransfer(dst_ids=ids, dma_engine_mask=mask, remote_sem=T.sem["arr" + tile],
+                                                  srcs=[side], dsts=[side] * len(dsts))], local_sem=T.sem.sent)
+            sent += len(engs)
     g.wait_ge(T.sem.sent, sent)

from concourse.bass import DstId, RemoteDMATransfer
from concourse.mybir import dt, AluOpType, ActivationFunctionType

NCOL = 128
W = 512
TILES = ["B", "T0", "T1", "T2", "T3", "T4", "T5", "P", "U", "V"]
SCRATCH = {
    "a_in": ("sbuf", [128, 4 * W], "bfloat16"),
    "b_in": ("sbuf", [128, W], "bfloat16"),
    "ones": ("sbuf", [128, W + 4], "bfloat16"),
    "pick": ("sbuf", [128, W + 4], "bfloat16"),
    "t_mid": ("sbuf", [128, W], "bfloat16"),
    "s_mid": ("sbuf", [128, W], "bfloat16"),
    "y_mid": ("sbuf", [128, W], "float32"),
    "ca": ("sbuf", [128, 4 * NCOL], "float8_e4m3fn_x4"),
    "pa": ("sbuf", [128, 4 * NCOL], "uint8"),
    "cs": ("sbuf", [128, 4 * NCOL], "float8_e4m3fn_x4"),
    "ps": ("sbuf", [128, 4 * NCOL], "uint8"),
    "acc0": ("psum", [128, 4 * 512], "float32"),
    "acc1": ("psum", [128, 4 * 512], "float32"),
}
for _t in TILES:
    SCRATCH["c" + _t] = ("sbuf", [128, NCOL], "float8_e4m3fn_x4")
    SCRATCH["p" + _t] = ("sbuf", [128, NCOL], "uint8")
STAGES = "tsy"
SEMAPHORES = ["la", "lb", "one", "sel", "qs", "qa", "stored", "sent"]
SEMAPHORES += ["q" + _t for _t in TILES] + ["arr" + _t for _t in TILES]
SEMAPHORES += ["%s%d" % (_s, _b) for _s in STAGES for _b in range(4)]
SEMAPHORES += ["%s_%s" % (_s, _e) for _s in STAGES for _e in ("act", "vec")]


def _roles(T, topo):
    cores = [int(c) for c in T.cores]
    root = cores[T.root]
    other = {c: [d for d in cores if d != c and topo.chip(d) == topo.chip(c)][0] for c in cores}
    peer = other[root]
    gates = [c for c in cores if c not in (root, peer) and all(topo.may_write(c, d) for d in cores if d != c)]
    near = [c for c in gates if topo.may_write(peer, c)][0]
    far = [c for c in gates if c != near][0]
    return root, peer, near, other[near], far, other[far]


def _plan(T, topo):
    root, peer, near, nspoke, far, fspoke = _roles(T, topo)
    t = {c: "T%d" % T.rank_of(c) for c in T.cores}

    def engines(src, dst):
        m = topo.mask(src, dst)
        return [e for e in range(16) if m >> e & 1]

    off = engines(root, near)
    inner = [e for e in engines(root, peer) if e not in off]
    sends = {
        root: [("B", [peer], off), ("B", [fspoke], off), ("B", [nspoke], off), ("B", [far], off),
               (t[root], [peer], inner)],
        peer: [("B", [near], off), ("P", [near], off), ("P", [nspoke], off), (t[peer], [root], off),
               ("U", [root], off)],
        nspoke: [(t[nspoke], [near], engines(nspoke, near)[::2]), (t[nspoke], [root], off), ("V", [peer], off)],
        fspoke: [(t[fspoke], [far], engines(fspoke, far)[::2])],
        near: [(t[near], [nspoke], off), (t[near], [root], off), ("V", [fspoke, far], off)],
        far: [(t[far], [fspoke], off), ("U", [peer], off), ("U", [nspoke, near], off)],
    }
    v = [t[near], t[nspoke], "P"]
    sums = {peer: ("P", [t[peer], t[root]]), near: ("V", v), nspoke: ("V", [t[nspoke], "P", t[near]]),
            far: ("U", [t[far], t[fspoke]])}
    ys = {root: [t[root], t[peer], t[nspoke], t[near], "U"], peer: ["U", "V"],
          near: v + ["U"], nspoke: [t[nspoke], "P", t[near], "U"],
          far: [t[far], t[fspoke], "V"], fspoke: [t[fspoke], t[far], "V"]}
    return sends, sums, ys


def rank_program(g, core, T, topo):
    rank = T.rank_of(core)
    if rank is None:
        return
    sends, sums, ys = _plan(T, topo)
    own = "T%d" % rank
    is_root = rank == T.root
    made = {own}
    if is_root:
        made.add("B")
    if core in sums:
        made.add(sums[core][0])
    arrive = {}
    for src in sends:
        for tile, dsts, engs in sends[src]:
            if core in dsts:
                arrive[tile] = 2 * len(engs)

    def codes(t):
        return T["c" + t][:, 0:NCOL]

    def plane(t):
        return T["p" + t][:, 0:NCOL]

    def have(q, t):
        if t in made:
            q.wait_ge(T.sem["q" + t], 1)
        else:
            q.wait_ge(T.sem["arr" + t], arrive[t])

    if is_root:
        g.sync.dma_start(T.b_in[:], T.b[:, :]).then_inc(T.sem.lb, 16)
    g.sync.dma_start(T.a_in[:], T.a[:, :]).then_inc(T.sem.la, 16)

    g.vector.memset(T.ones[:], 1.0).then_inc(T.sem.one, 1)
    g.wait_ge(T.sem.one, 1)
    g.affine_select(T.pick[:], T.ones[:], [[-1, W + 4]], AluOpType.is_equal, 0.0, 3, 4).then_inc(T.sem.sel, 1)

    if is_root:
        g.vector.wait_ge(T.sem.lb, 16)
        g.vector.quantize_mx(codes("B"), plane("B"), T.b_in[:]).then_inc(T.sem.qB, 1)
    g.vector.wait_ge(T.sem.sel, 1)
    for b in range(4):
        c0 = b * NCOL
        g.vector.quantize_mx(T.cs[:, c0:c0 + NCOL], T.ps[:, c0:c0 + NCOL], T.pick[:, 3 - b:3 - b + W]).then_inc(T.sem.qs, 1)
    g.vector.wait_ge(T.sem.la, 16)
    g.vector.quantize_mx(T.ca[:], T.pa[:], T.a_in[:]).then_inc(T.sem.qa, 1)

    def bank(acc, b):
        return acc[:, 512 * b:512 * b + NCOL]

    def leave(stage, acc, out, clamp):
        for b in (0, 2):
            g.scalar.wait_ge(T.sem["%s%d" % (stage, b)], 1)
            f = ActivationFunctionType.Relu if clamp else ActivationFunctionType.Copy
            g.scalar.activation(out[:, b:W:4], bank(acc, b), f).then_inc(T.sem[stage + "_act"], 1)
        for b in (1, 3):
            g.vector.wait_ge(T.sem["%s%d" % (stage, b)], 1)
            if clamp:
                call = g.vector.tensor_scalar(out[:, b:W:4], bank(acc, b), 0.0, None, AluOpType.max)
            else:
                call = g.vector.tensor_copy(out[:, b:W:4], bank(acc, b))
            call.then_inc(T.sem[stage + "_vec"], 1)

    def quantise(stage, tile, mid):
        g.vector.wait_ge(T.sem[stage + "_vec"], 2)
        g.vector.wait_ge(T.sem[stage + "_act"], 2)
        g.vector.quantize_mx(codes(tile), plane(tile), mid[:]).then_inc(T.sem["q" + tile], 1)

    g.tensor.wait_ge(T.sem.qa, 1)
    have(g.tensor, "B")
    for b in range(4):
        c0 = b * NCOL
        g.tensor.matmul_mx(bank(T.acc0, b), T.ca[:, c0:c0 + NCOL], T.pa[:, c0:c0 + NCOL], codes("B"), plane("B"),
                           True, True).then_inc(T.sem["t%d" % b], 1)
    leave("t", T.acc0, T.t_mid, True)
    quantise("t", own, T.t_mid)
    have(g.tensor, own)
    g.tensor.wait_ge(T.sem.qs, 4)

    seen = {own}

    def add_up(stage, acc, parts):
        for k, t in enumerate(parts):
            if t not in seen:
                seen.add(t)
                have(g.tensor, t)
            for b in range(4):
                c0 = b * NCOL
                call = g.tensor.matmul_mx(bank(acc, b), T.cs[:, c0:c0 + NCOL], T.ps[:, c0:c0 + NCOL], codes(t), plane(t),
                                          k == 0, k == len(parts) - 1)
                if k == len(parts) - 1:
                    call.then_inc(T.sem["%s%d" % (stage, b)], 1)

    if core in sums:
        add_up("s", T.acc1, sums[core][1])
        leave("s", T.acc1, T.s_mid, False)
        quantise("s", sums[core][0], T.s_mid)

    add_up("y", T.acc0, ys[core])
    leave("y", T.acc0, T.y_mid, False)
    g.sync.wait_ge(T.sem.y_act, 2)
    g.sync.wait_ge(T.sem.y_vec, 2)
    g.sync.dma_start(T.y[:, :], T.y_mid[:]).then_inc(T.sem.stored, 16)
    g.sync.wait_ge(T.sem.stored, 16)

    sent = 0
    held = set()
    for tile, dsts, engs in sends[core]:
        if tile not in held:
            held.add(tile)
            have(g, tile)
        ids = []
        for d in dsts:
            rid, pid, _s = topo.addr(d)
            ids.append(DstId(rid=rid, pnc=pid))
        mask = sum(1 << e for e in engs)
        for side in (codes(tile).bitcast(dt.uint8), plane(tile)):
            g.remote_dma_fused([RemoteDMATransfer(dst_ids=ids, dma_engine_mask=mask, remote_sem=T.sem["arr" + tile],
                                                  srcs=[side], dsts=[side] * len(dsts))], local_sem=T.sem.sent)
            sent += len(engs)
    g.wait_ge(T.sem.sent, sent)
